import numpy as np
import ml_dtypes


def mxq(x, axis, fmt="e4m3"):
    dtype, down = {"e4m3": (ml_dtypes.float8_e4m3fn, 7), "e5m2": (ml_dtypes.float8_e5m2, 14)}[fmt]
    v = np.moveaxis(np.asarray(x, np.float32).astype(ml_dtypes.bfloat16).astype(np.float64), axis, -1)
    blocks = v.reshape(v.shape[:-1] + (-1, 32))
    amax = np.abs(blocks).max(-1, keepdims=True)
    byte = np.maximum(np.where(amax > 0, np.frexp(amax)[1] - 1 + 127, 0) - down, 1)
    scale = np.exp2(byte - 127.0)
    codes = (blocks / scale).astype(np.float32).astype(dtype).astype(np.float64)
    return np.moveaxis((codes * scale).reshape(v.shape), -1, axis)


WIDE = False


def mx_kscale(k):
    if not WIDE:
        return np.ones(k)
    levels = np.array([10, -10, 5, -5, 0])
    if k % 512:
        return np.exp2(np.random.permutation(np.resize(levels, k // 32))).repeat(32)
    a = np.empty((k // 512, 16))
    for p in range(k // 512):
        a[p, :8] = np.random.permutation(np.resize(levels, 8))
        for g in range(8):
            far = levels[np.abs(levels - a[p, g]) >= 10]
            a[p, g + 8] = far[np.random.randint(len(far))]
    return np.exp2(a.ravel()).repeat(32)


def f64(x):
    return np.asarray(x).astype(np.float64)


def striped(idx):
    return np.tile(idx.reshape(-1, 16).T, (8, 1)).astype(np.uint16)


def unstriped(offs):
    return offs[:16].T.reshape(-1).astype(np.int64)


def striped8(idx):
    return np.concatenate([x.reshape(-1, 16).T for x in idx]).astype(np.uint16)


def runs(offs, k):
    lists = np.stack([offs[16 * r : 16 * r + 16].T.reshape(-1) for r in range(8)]).astype(np.int64)
    return lists[np.arange(k) % 512 // 64]


def pack_weight(w):
    k, n = w.shape
    w = f64(np.asarray(w, np.float32).astype(ml_dtypes.bfloat16)).reshape(k // 32, 32, n)
    amax = np.abs(w).max(1)
    byte = np.clip(np.where(amax > 0, np.frexp(amax)[1] - 1 + 127 - 7, 1), 1, 254)
    scaled = (w * np.exp2(127.0 - byte)[:, None, :]).reshape(k, n).astype(np.float32)
    words = np.ascontiguousarray(scaled.reshape(k // 512, 128, 4, n).transpose(0, 1, 3, 2)).astype(ml_dtypes.float8_e4m3fn).view(np.uint8)
    return words, np.ascontiguousarray(byte.astype(np.uint8).reshape(k // 512, 16, n))


def unpack_weight(words, scales):
    g, p, n, _ = words.shape
    vals = np.ascontiguousarray(words).view(ml_dtypes.float8_e4m3fn).astype(np.float64) * np.repeat(np.exp2(scales.astype(np.float64) - 127.0), 8, axis=1)[..., None]
    return vals.transpose(0, 1, 3, 2).reshape(g * 512, n)


E2M1 = np.array([0.0, 0.5, 1.0, 1.5, 2.0, 3.0, 4.0, 6.0, -0.0, -0.5, -1.0, -1.5, -2.0, -3.0, -4.0, -6.0])


def pack_fp4(w):
    k, n = w.shape
    w = f64(np.asarray(w, np.float32).astype(ml_dtypes.bfloat16)).reshape(k // 32, 32, n)
    amax = np.abs(w).max(1)
    mant, ex = np.frexp(amax / 6.0)
    byte = np.clip(np.where(amax > 0, np.where(mant > 0.5, ex, ex - 1) + 127, 1), 1, 254)
    scaled = (w * np.exp2(127.0 - byte)[:, None, :]).reshape(k, n).astype(np.float32)
    c = np.ascontiguousarray(scaled.reshape(k // 512, 128, 4, n).transpose(0, 1, 3, 2)).astype(ml_dtypes.float4_e2m1fn).view(np.uint8) & 0xF
    words = (c[..., 0::2] | (c[..., 1::2] << 4)).reshape(k // 512, 128, 2 * n)
    return np.ascontiguousarray(words), np.ascontiguousarray(byte.astype(np.uint8).reshape(k // 512, 16, n))


def unpack_fp4(words, scales):
    g, _, n = scales.shape
    words = np.ascontiguousarray(words).reshape(g, 128, n, 2)
    nib = np.empty((g, 128, n, 4), np.uint8)
    nib[..., 0::2] = words & 0xF
    nib[..., 1::2] = words >> 4
    vals = E2M1[nib] * np.repeat(np.exp2(scales.astype(np.float64) - 127.0), 8, axis=1)[..., None]
    return vals.transpose(0, 1, 3, 2).reshape(g * 512, n)


def sigmoid(v):
    return 1.0 / (1.0 + np.exp(-np.maximum(v, -700.0)))

def planes(y):
    n, m = y.shape
    v = y.astype(np.float32).astype(ml_dtypes.bfloat16).astype(np.float64).reshape(n // 32, 32, m)
    top = np.abs(v).max(1)
    byte = np.clip(np.where(top > 0, np.frexp(top)[1] - 1 + 127 - 7, 1), 1, 254)
    codes = (v * np.exp2(127.0 - byte)[:, None, :]).reshape(n, m).astype(np.float32).astype(ml_dtypes.float8_e4m3fn).view(np.uint8)
    words = codes.reshape(n // 512, 128, 4, m).transpose(0, 1, 3, 2)
    return np.ascontiguousarray(words), np.ascontiguousarray(byte.astype(np.uint8).reshape(n // 512, 16, m))


K, T, S, H, G, J = 512, 2048, 512, 512, 2048, 512


def setup_inputs():
    n = np.random.standard_normal
    s = mx_kscale(K)[:, None]
    packed_xT = pack_weight(n((K, T)) * s)
    packed_w1 = pack_fp4(n((K, H)) / np.sqrt(K) / s)
    packed_dT = pack_weight(n((K, G)) / s)
    return {
        "x_words": packed_xT[0],
        "x_scales": packed_xT[1],
        "w1_words": packed_w1[0],
        "w1_scales": packed_w1[1],
        "gs": (np.random.uniform(0.5, 1.5, (K, 1)) * s).astype(np.float32),
        "d_words": packed_dT[0],
        "d_scales": packed_dT[1],
        "tab": n((H, J)).astype(np.float32),
        "offs": striped(np.random.permutation(T)[:S]),
        "n1": striped8(np.stack([np.random.permutation(S) for _ in range(8)])),
        "n2": striped8(np.stack([np.random.permutation(S) for _ in range(8)])),
        "n3": striped8(np.stack([np.random.permutation(S) for _ in range(8)])),
        "k1": striped8(np.random.randint(0, G, (8, H))),
        "n4": striped8(np.random.randint(0, J, (8, S))),
        "n5": striped8(np.random.randint(0, J, (8, S))),
        "n6": striped8(np.stack([np.random.permutation(S) for _ in range(8)])),
    }


def reference(x_words, x_scales, w1_words, w1_scales, gs, d_words, d_scales, tab, offs, n1, n2, n3, k1, n4, n5, n6):
    d_k1 = unpack_weight(d_words, d_scales)[np.arange(K)[:, None], runs(k1, K)]
    xq = unpack_weight(x_words, x_scales)[:, unstriped(offs)]
    y = unpack_fp4(w1_words, w1_scales).T @ xq
    z = f64(gs) * ((y[np.arange(H)[:, None], runs(n1, H)]) * sigmoid(y) + (y[np.arange(H)[:, None], runs(n2, H)]) * (sigmoid(y[np.arange(H)[:, None], runs(n3, H)])))
    h = 0.0625 * ((d_k1.T @ mxq(z, 0, "e4m3")))
    out_0 = (h[np.arange(H)[:, None], runs(n6, H)]) * (f64(tab)[np.arange(H)[:, None], runs(n4, H)]) + f64(tab)[np.arange(H)[:, None], runs(n5, H)]
    return (out_0,) + planes(out_0)

@@ -1,0 +1,207 @@
+from contextlib import ExitStack
+
+import concourse.mybir as mybir
+
+K, T, S, H, G, J = 512, 2048, 512, 512, 2048, 512
+FLOPS = 2 * K * H * S + 2 * H * H * S
+
+F32 = mybir.dt.float32
+BF16 = mybir.dt.bfloat16
+I32 = mybir.dt.int32
+U32 = mybir.dt.uint32
+U16 = mybir.dt.uint16
+U8 = mybir.dt.uint8
+FP8X4 = mybir.dt.float8_e4m3fn_x4
+FP4X4 = mybir.dt.float4_e2m1fn_x4
+MULT = mybir.AluOpType.mult
+ADD = mybir.AluOpType.add
+COPY = mybir.ActivationFunctionType.Copy
+SIGMOID = mybir.ActivationFunctionType.Sigmoid
+
+P = 128
+PACK = 4
+WINDOW = 1024
+OUT_CHUNKS = ((0, 256), (256, 512))
+
+
+def tile_picked_densewsumkinda_none_po_kernel(
+    tc, x_words, x_scales, w1_words, w1_scales, gs, d_words, d_scales, tab,
+    offs, n1, n2, n3, k1, n4, n5, n6, out_0, out_1, out_2,
+):
+    nc = tc.nc
+    with ExitStack() as ctx:
+        lists = ctx.enter_context(tc.tile_pool(name="lists", bufs=1))
+        keep = ctx.enter_context(tc.tile_pool(name="keep", bufs=1))
+        psum = ctx.enter_context(tc.psum_pool(name="psum", bufs=1))
+
+        def list_tile(name):
+            return lists.tile([P, S // 16], U16, name=name)
+
+        def tiles(name, shape, dtype):
+            return [keep.tile(shape, dtype, name=name + str(t), align_bytes=64) for t in range(PACK)]
+
+        offs_sb, k1_sb = list_tile("offs_sb"), list_tile("k1_sb")
+        n1_sb, n2_sb, n3_sb = list_tile("n1_sb"), list_tile("n2_sb"), list_tile("n3_sb")
+        n4_sb, n5_sb, n6_sb = list_tile("n4_sb"), list_tile("n5_sb"), list_tile("n6_sb")
+
+        xw = keep.tile([P, T], I32, align_bytes=64)
+        xs = keep.tile([P, T], U8, align_bytes=64)
+        w1w = keep.tile([P, 2 * H], U8, align_bytes=64)
+        w1s = keep.tile([P, H], U8, align_bytes=64)
+        dw = keep.tile([P, G], I32, align_bytes=64)
+        ds = keep.tile([P, G], U8, align_bytes=64)
+        dsf = keep.tile([P, H], U8, align_bytes=64)
+        gs_sb = keep.tile([P, PACK], F32, align_bytes=64)
+        warm = keep.tile([P, 2], F32, align_bytes=64)
+        tab_w = tiles("tab_w", [P, WINDOW], F32)
+        y_w = tiles("y_w", [P, WINDOW], F32)
+        yg_w = tiles("yg_w", [P, WINDOW], F32)
+        h_w = tiles("h_w", [P, WINDOW], F32)
+
+        nc.gpsimd.memset(xs[:].bitcast(I32), 0)
+        nc.vector.memset(w1s[:].bitcast(I32), 0)
+        nc.vector.memset(ds[:].bitcast(I32), 0)
+        nc.vector.memset(warm[:, 0:1], 0.0)
+        nc.scalar.activation(warm[:, 1:2], warm[:, 0:1], SIGMOID)
+        tab_rows = tab.rearrange("(p t) j -> p t j", t=PACK)
+        nc.sync.dma_start(tab_w[0][:, :J], tab_rows[:, 0, :])
+        for q in range(4):
+            nc.sync.dma_start(xs[32 * q : 32 * q + 4, :].bitcast(I32), x_scales[0, 4 * q : 4 * q + 4, :].bitcast(I32))
+        nc.sync.dma_start(n4_sb[:], n4)
+        nc.sync.dma_start(offs_sb[:], offs)
+        nc.sync.dma_start(w1w[:].bitcast(I32), w1_words[0].bitcast(I32))
+        nc.sync.dma_start(xw[:], x_words[0].rearrange("p n t -> p (n t)").bitcast(I32))
+        for q in range(4):
+            nc.sync.dma_start(w1s[32 * q : 32 * q + 4, :].bitcast(I32), w1_scales[0, 4 * q : 4 * q + 4, :].bitcast(I32))
+        nc.gpsimd.dma_start(gs_sb[:], gs.rearrange("(p t) o -> p (t o)", t=PACK))
+        for e in range(2):
+            nc.gpsimd.dma_start(ds[e:P:16, :].bitcast(I32), d_scales[0, e:16:2, :].bitcast(I32))
+        nc.sync.dma_start(k1_sb[:], k1)
+        nc.sync.dma_start(tab_w[1][:, :J], tab_rows[:, 1, :])
+        nc.sync.dma_start(n1_sb[:], n1)
+        nc.sync.dma_start(n3_sb[:], n3)
+        nc.sync.dma_start(dw[:], d_words[0].rearrange("p n t -> p (n t)").bitcast(I32))
+        nc.sync.dma_start(n2_sb[:], n2)
+        nc.sync.dma_start(tab_w[2][:, :J], tab_rows[:, 2, :])
+        nc.sync.dma_start(tab_w[3][:, :J], tab_rows[:, 3, :])
+        nc.sync.dma_start(n6_sb[:], n6)
+        nc.sync.dma_start(n5_sb[:], n5)
+
+        xsg = keep.tile([P, S], U8, align_bytes=64)
+        xg = keep.tile([P, S], U32, align_bytes=64)
+        w1d = keep.tile([P, 2 * H], U8, align_bytes=64)
+        w1sd = keep.tile([P, H], U8, align_bytes=64)
+        t4_early = [keep.tile([P, S], F32, name="t4_" + str(t), align_bytes=64) for t in range(2)]
+        nc.vector.tensor_copy(t4_early[0][:], tab_w[0][:].indirect(n4_sb[:]))
+        nc.vector.tensor_copy(xsg[:], xs[:].indirect(offs_sb[:]))
+        nc.vector.tensor_copy(
+            w1d[:].rearrange("p (t m b) -> p t m b", t=PACK, b=2),
+            w1w[:].rearrange("p (m t b) -> p t m b", t=PACK, b=2),
+        )
+        nc.vector.tensor_copy(
+            w1sd[:].rearrange("p (t m) -> p t m", t=PACK),
+            w1s[:].rearrange("p (m t) -> p t m", t=PACK),
+        )
+        nc.vector.tensor_copy(xg[:], xw[:].bitcast(U32).indirect(offs_sb[:]))
+        nc.vector.tensor_copy(t4_early[1][:], tab_w[1][:].indirect(n4_sb[:]))
+        y_ps = [psum.tile([P, S], F32, name="y_ps" + str(t)) for t in range(PACK)]
+        for t in range(PACK):
+            nc.tensor.matmul_mx(
+                out=y_ps[t][:],
+                lhsT=w1d[:, 2 * P * t : 2 * P * (t + 1)].bitcast(FP4X4),
+                lhsT_scale=w1sd[:, P * t : P * (t + 1)],
+                rhs=xg[:].bitcast(FP8X4),
+                rhs_scale=xsg[:],
+                start=True,
+                stop=True,
+            )
+
+        s3 = tiles("s3", [P, S], F32)
+        term_a = keep.tile([P, PACK, S], F32, align_bytes=64)
+        term_b = keep.tile([P, PACK, S], F32, align_bytes=64)
+        t4 = [t4_early[0][:], t4_early[1][:], term_a[:, 0, :], term_a[:, 1, :]]
+        dg = keep.tile([P, H], U32, align_bytes=64)
+        dsg = keep.tile([P, H], U8, align_bytes=64)
+        dd = keep.tile([P, H], I32, align_bytes=64)
+        dsd = keep.tile([P, H], U8, align_bytes=64)
+
+        for t in range(PACK):
+            nc.scalar.activation(yg_w[t][:, :S], y_ps[t][:], COPY, scale=gs_sb[:, t : t + 1])
+            nc.scalar.activation(y_w[t][:, S:], y_ps[t][:], SIGMOID)
+            nc.scalar.activation(y_w[t][:, :S], y_ps[t][:], COPY)
+            nc.scalar.activation(s3[t][:], y_w[t][:].indirect(n3_sb[:]), SIGMOID)
+            nc.vector.tensor_tensor(term_a[:, t, :], yg_w[t][:].indirect(n1_sb[:]), y_w[t][:, S:], MULT)
+            nc.vector.tensor_tensor(term_b[:, t, :], yg_w[t][:].indirect(n2_sb[:]), s3[t][:], MULT)
+
+        nc.vector.tensor_copy(dsg[:], ds[:].indirect(k1_sb[:]))
+        nc.vector.tensor_copy(dg[:], dw[:].bitcast(U32).indirect(k1_sb[:]))
+        nc.vector.tensor_copy(
+            dsd[:].rearrange("p (t m) -> p t m", t=PACK),
+            dsg[:].rearrange("p (m t) -> p t m", t=PACK),
+        )
+        nc.vector.tensor_copy(
+            dd[:].rearrange("p (t m) -> p t m", t=PACK),
+            dg[:].bitcast(I32).rearrange("p (m t) -> p t m", t=PACK),
+        )
+        for r in range(4):
+            first = 16 * (r // 2) + r % 2
+            nc.sync.dma_start(dsf[r:P:32, :].bitcast(I32), dsd[first:P:32, :].bitcast(I32))
+
+        zb = keep.tile([P, S, PACK], BF16, align_bytes=64)
+        zq = keep.tile([P, S], U32, align_bytes=64)
+        zs = keep.tile([P, S], U8, align_bytes=64)
+        half = S // 2
+        for a in (0, half):
+            nc.vector.tensor_tensor(
+                zb[:, a : a + half, :].rearrange("p (c i) t -> p c t i", i=4),
+                term_a[:, :, a : a + half].rearrange("p t (c i) -> p c t i", i=4),
+                term_b[:, :, a : a + half].rearrange("p t (c i) -> p c t i", i=4),
+                ADD,
+            )
+        for a in (0, half):
+            nc.vector.quantize_mx(
+                out=zq[:, a : a + half].bitcast(FP8X4),
+                scales=zs[:, a : a + half],
+                in_=zb[:, a : a + half, :].rearrange("p s t -> p (s t)"),
+            )
+        for t in (2, 3):
+            nc.vector.tensor_copy(t4[t], tab_w[t][:].indirect(n4_sb[:]))
+
+        h_ps = [psum.tile([P, S], F32, name="h_ps" + str(t)) for t in range(PACK)]
+        for t in range(PACK):
+            nc.tensor.matmul_mx(
+                out=h_ps[t][:],
+                lhsT=dd[:, P * t : P * (t + 1)].bitcast(FP8X4),
+                lhsT_scale=dsf[:, P * t : P * (t + 1)],
+                rhs=zq[:].bitcast(FP8X4),
+                rhs_scale=zs[:],
+                start=True,
+                stop=True,
+            )
+            nc.scalar.activation(h_w[t][:, :S], h_ps[t][:], COPY, scale=0.0625)
+
+        out_rows = out_0.rearrange("(p t) s -> p t s", t=PACK)
+        oq = keep.tile([P, S], I32, align_bytes=64)
+        osc = keep.tile([P, S], U8, align_bytes=64)
+        out_words = out_1[0].rearrange("p n t -> p (n t)").bitcast(I32)
+        for c, (a, b) in enumerate(OUT_CHUNKS):
+            n = b - a
+            prod = keep.tile([P, PACK, n], F32, name="prod" + str(c), align_bytes=64)
+            res = keep.tile([P, PACK, n], F32, name="res" + str(c), align_bytes=64)
+            ob = keep.tile([P, n, PACK], BF16, name="ob" + str(c), align_bytes=64)
+            for t in range(PACK):
+                nc.vector.tensor_tensor(prod[:, t, :], h_w[t][:].indirect(n6_sb[:, a // 16 : b // 16]), t4[t][:, a:b], MULT)
+            for t in range(PACK):
+                nc.vector.tensor_tensor(res[:, t, :], tab_w[t][:].indirect(n5_sb[:, a // 16 : b // 16]), prod[:, t, :], ADD)
+                nc.sync.dma_start(out_rows[:, t, a:b], res[:, t, :])
+            dst = ob[:].rearrange("p (c i) t -> p c t i", i=4)
+            src = res[:].rearrange("p t (c i) -> p c t i", i=4)
+            if c + 1 < len(OUT_CHUNKS):
+                nc.scalar.copy(dst, src)
+            else:
+                nc.vector.tensor_copy(dst, src)
+            nc.vector.quantize_mx(out=oq[:, a:b].bitcast(FP8X4), scales=osc[:, a:b], in_=ob[:].rearrange("p s t -> p (s t)"))
+            nc.sync.dma_start(out_words[:, a:b], oq[:, a:b])
+        for q in range(4):
+            eng = nc.scalar if q % 2 else nc.sync
+            eng.dma_start(out_2[0, 4 * q : 4 * q + 4, :].bitcast(I32), osc[32 * q : 32 * q + 4, :].bitcast(I32))

@@ -44,7 +44,7 @@ def tile_picked_densewsumkinda_none_po_kernel(
         n1_sb, n2_sb, n3_sb = list_tile("n1_sb"), list_tile("n2_sb"), list_tile("n3_sb")
         n4_sb, n5_sb, n6_sb = list_tile("n4_sb"), list_tile("n5_sb"), list_tile("n6_sb")
 
-        xw = keep.tile([P, T], I32, align_bytes=64)
+        xw = keep.tile([P, T], I32, tag="xw", align_bytes=64)
         xs = keep.tile([P, T], U8, align_bytes=64)
         w1w = keep.tile([P, 2 * H], U8, align_bytes=64)
         w1s = keep.tile([P, H], U8, align_bytes=64)
@@ -58,31 +58,31 @@ def tile_picked_densewsumkinda_none_po_kernel(
         yg_w = tiles("yg_w", [P, WINDOW], F32)
         h_w = tiles("h_w", [P, WINDOW], F32)
 
-        nc.gpsimd.memset(xs[:].bitcast(I32), 0)
+        nc.vector.memset(xs[:].bitcast(I32), 0)
         nc.vector.memset(w1s[:].bitcast(I32), 0)
-        nc.vector.memset(ds[:].bitcast(I32), 0)
+        nc.gpsimd.memset(ds[:].bitcast(I32), 0)
         nc.vector.memset(warm[:, 0:1], 0.0)
         nc.scalar.activation(warm[:, 1:2], warm[:, 0:1], SIGMOID)
         tab_rows = tab.rearrange("(p t) j -> p t j", t=PACK)
+        nc.sync.dma_start(n4_sb[:], n4)
         nc.sync.dma_start(tab_w[0][:, :J], tab_rows[:, 0, :])
+        nc.sync.dma_start(w1w[:].bitcast(I32), w1_words[0].bitcast(I32))
+        nc.sync.dma_start(tab_w[1][:, :J], tab_rows[:, 1, :])
+        nc.sync.dma_start(offs_sb[:], offs)
+        nc.sync.dma_start(xw[:], x_words[0].rearrange("p n t -> p (n t)").bitcast(I32))
         for q in range(4):
             nc.sync.dma_start(xs[32 * q : 32 * q + 4, :].bitcast(I32), x_scales[0, 4 * q : 4 * q + 4, :].bitcast(I32))
-        nc.sync.dma_start(n4_sb[:], n4)
-        nc.sync.dma_start(offs_sb[:], offs)
-        nc.sync.dma_start(w1w[:].bitcast(I32), w1_words[0].bitcast(I32))
-        nc.sync.dma_start(xw[:], x_words[0].rearrange("p n t -> p (n t)").bitcast(I32))
         for q in range(4):
             nc.sync.dma_start(w1s[32 * q : 32 * q + 4, :].bitcast(I32), w1_scales[0, 4 * q : 4 * q + 4, :].bitcast(I32))
         nc.gpsimd.dma_start(gs_sb[:], gs.rearrange("(p t) o -> p (t o)", t=PACK))
         for e in range(2):
             nc.gpsimd.dma_start(ds[e:P:16, :].bitcast(I32), d_scales[0, e:16:2, :].bitcast(I32))
+        nc.sync.dma_start(tab_w[2][:, :J], tab_rows[:, 2, :])
         nc.sync.dma_start(k1_sb[:], k1)
-        nc.sync.dma_start(tab_w[1][:, :J], tab_rows[:, 1, :])
         nc.sync.dma_start(n1_sb[:], n1)
         nc.sync.dma_start(n3_sb[:], n3)
         nc.sync.dma_start(dw[:], d_words[0].rearrange("p n t -> p (n t)").bitcast(I32))
         nc.sync.dma_start(n2_sb[:], n2)
-        nc.sync.dma_start(tab_w[2][:, :J], tab_rows[:, 2, :])
         nc.sync.dma_start(tab_w[3][:, :J], tab_rows[:, 3, :])
         nc.sync.dma_start(n6_sb[:], n6)
         nc.sync.dma_start(n5_sb[:], n5)
@@ -93,18 +93,20 @@ def tile_picked_densewsumkinda_none_po_kernel(
         w1sd = keep.tile([P, H], U8, align_bytes=64)
         t4_early = [keep.tile([P, S], F32, name="t4_" + str(t), align_bytes=64) for t in range(2)]
         nc.vector.tensor_copy(t4_early[0][:], tab_w[0][:].indirect(n4_sb[:]))
+        nc.vector.tensor_copy(
+            w1d[:].rearrange("p (t c i b) -> p c t i b", t=PACK, i=8, b=2),
+            w1w[:].rearrange("p (c i t b) -> p c t i b", t=PACK, i=8, b=2),
+        )
+        nc.vector.tensor_copy(t4_early[1][:], tab_w[1][:].indirect(n4_sb[:]))
+        nc.vector.tensor_copy(xg[:], xw[:].bitcast(U32).indirect(offs_sb[:]))
         nc.vector.tensor_copy(xsg[:], xs[:].indirect(offs_sb[:]))
         nc.vector.tensor_copy(
-            w1d[:].rearrange("p (t m b) -> p t m b", t=PACK, b=2),
-            w1w[:].rearrange("p (m t b) -> p t m b", t=PACK, b=2),
+            w1sd[:].rearrange("p (t c i) -> p c t i", t=PACK, i=16),
+            w1s[:].rearrange("p (c i t) -> p c t i", t=PACK, i=16),
         )
-        nc.vector.tensor_copy(
-            w1sd[:].rearrange("p (t m) -> p t m", t=PACK),
-            w1s[:].rearrange("p (m t) -> p t m", t=PACK),
-        )
-        nc.vector.tensor_copy(xg[:], xw[:].bitcast(U32).indirect(offs_sb[:]))
-        nc.vector.tensor_copy(t4_early[1][:], tab_w[1][:].indirect(n4_sb[:]))
-        y_ps = [psum.tile([P, S], F32, name="y_ps" + str(t)) for t in range(PACK)]
+        t4_early.append(keep.tile([P, S], F32, name="t4_2", tag="xw", align_bytes=64))
+        nc.vector.tensor_copy(t4_early[2][:], tab_w[2][:].indirect(n4_sb[:]))
+        y_ps = [psum.tile([P, S], F32, name="y_ps", tag="bank" + str(t)) for t in range(PACK)]
         for t in range(PACK):
             nc.tensor.matmul_mx(
                 out=y_ps[t][:],
@@ -119,29 +121,30 @@ def tile_picked_densewsumkinda_none_po_kernel(
         s3 = tiles("s3", [P, S], F32)
         term_a = keep.tile([P, PACK, S], F32, align_bytes=64)
         term_b = keep.tile([P, PACK, S], F32, align_bytes=64)
-        t4 = [t4_early[0][:], t4_early[1][:], term_a[:, 0, :], term_a[:, 1, :]]
+        t4 = [t4_early[0][:], t4_early[1][:], t4_early[2][:], term_a[:, 0, :]]
         dg = keep.tile([P, H], U32, align_bytes=64)
         dsg = keep.tile([P, H], U8, align_bytes=64)
         dd = keep.tile([P, H], I32, align_bytes=64)
         dsd = keep.tile([P, H], U8, align_bytes=64)
 
+        sig = tiles("sig", [P, S], F32)
         for t in range(PACK):
-            nc.scalar.activation(yg_w[t][:, :S], y_ps[t][:], COPY, scale=gs_sb[:, t : t + 1])
-            nc.scalar.activation(y_w[t][:, S:], y_ps[t][:], SIGMOID)
             nc.scalar.activation(y_w[t][:, :S], y_ps[t][:], COPY)
+            nc.scalar.activation(yg_w[t][:, :S], y_ps[t][:], COPY, scale=gs_sb[:, t : t + 1])
+            nc.scalar.activation(sig[t][:], y_ps[t][:], SIGMOID)
             nc.scalar.activation(s3[t][:], y_w[t][:].indirect(n3_sb[:]), SIGMOID)
-            nc.vector.tensor_tensor(term_a[:, t, :], yg_w[t][:].indirect(n1_sb[:]), y_w[t][:, S:], MULT)
+            nc.vector.tensor_tensor(term_a[:, t, :], yg_w[t][:].indirect(n1_sb[:]), sig[t][:], MULT)
             nc.vector.tensor_tensor(term_b[:, t, :], yg_w[t][:].indirect(n2_sb[:]), s3[t][:], MULT)
 
         nc.vector.tensor_copy(dsg[:], ds[:].indirect(k1_sb[:]))
         nc.vector.tensor_copy(dg[:], dw[:].bitcast(U32).indirect(k1_sb[:]))
         nc.vector.tensor_copy(
-            dsd[:].rearrange("p (t m) -> p t m", t=PACK),
-            dsg[:].rearrange("p (m t) -> p t m", t=PACK),
+            dsd[:].rearrange("p (t c i) -> p c t i", t=PACK, i=16),
+            dsg[:].rearrange("p (c i t) -> p c t i", t=PACK, i=16),
         )
         nc.vector.tensor_copy(
-            dd[:].rearrange("p (t m) -> p t m", t=PACK),
-            dg[:].bitcast(I32).rearrange("p (m t) -> p t m", t=PACK),
+            dd[:].rearrange("p (t c i) -> p c t i", t=PACK, i=4),
+            dg[:].bitcast(I32).rearrange("p (c i t) -> p c t i", t=PACK, i=4),
         )
         for r in range(4):
             first = 16 * (r // 2) + r % 2
@@ -164,44 +167,54 @@ def tile_picked_densewsumkinda_none_po_kernel(
                 scales=zs[:, a : a + half],
                 in_=zb[:, a : a + half, :].rearrange("p s t -> p (s t)"),
             )
-        for t in (2, 3):
+        for t in (3,):
             nc.vector.tensor_copy(t4[t], tab_w[t][:].indirect(n4_sb[:]))
 
-        h_ps = [psum.tile([P, S], F32, name="h_ps" + str(t)) for t in range(PACK)]
-        for t in range(PACK):
+        pieces = [(0, 0, half), (0, half, S)] + [(t, 0, S) for t in range(1, PACK)]
+        for i, (t, a, b) in enumerate(pieces):
+            h_ps = psum.tile([P, S], F32, name="h_ps", tag="bank" + str((i + PACK) % 8))
             nc.tensor.matmul_mx(
-                out=h_ps[t][:],
+                out=h_ps[:, a:b],
                 lhsT=dd[:, P * t : P * (t + 1)].bitcast(FP8X4),
                 lhsT_scale=dsf[:, P * t : P * (t + 1)],
-                rhs=zq[:].bitcast(FP8X4),
-                rhs_scale=zs[:],
+                rhs=zq[:, a:b].bitcast(FP8X4),
+                rhs_scale=zs[:, a:b],
                 start=True,
                 stop=True,
             )
-            nc.scalar.activation(h_w[t][:, :S], h_ps[t][:], COPY, scale=0.0625)
+            nc.scalar.activation(h_w[t][:, a:b], h_ps[:, a:b], COPY, scale=0.0625)
 
+        prod = keep.tile([P, PACK, S], F32, align_bytes=64)
+        for t in range(PACK):
+            nc.vector.tensor_tensor(prod[:, t, :], h_w[t][:].indirect(n6_sb[:]), t4[t], MULT)
         out_rows = out_0.rearrange("(p t) s -> p t s", t=PACK)
         oq = keep.tile([P, S], I32, align_bytes=64)
         osc = keep.tile([P, S], U8, align_bytes=64)
         out_words = out_1[0].rearrange("p n t -> p (n t)").bitcast(I32)
-        for c, (a, b) in enumerate(OUT_CHUNKS):
-            n = b - a
-            prod = keep.tile([P, PACK, n], F32, name="prod" + str(c), align_bytes=64)
-            res = keep.tile([P, PACK, n], F32, name="res" + str(c), align_bytes=64)
-            ob = keep.tile([P, n, PACK], BF16, name="ob" + str(c), align_bytes=64)
+        res = [keep.tile([P, PACK, half], F32, name="res" + str(c), align_bytes=64) for c in range(2)]
+        ob = [keep.tile([P, half, PACK], BF16, name="ob" + str(c), align_bytes=64) for c in range(2)]
+
+        def weave(copy, c, a, b):
+            copy(
+                ob[c][:, a:b, :].rearrange("p (g i) t -> p g t i", i=4),
+                res[c][:, :, a:b].rearrange("p t (g i) -> p g t i", i=4),
+            )
+
+        def quantize_out(c):
+            cols = slice(c * half, (c + 1) * half)
+            nc.vector.quantize_mx(out=oq[:, cols].bitcast(FP8X4), scales=osc[:, cols], in_=ob[c][:].rearrange("p s t -> p (s t)"))
+            nc.sync.dma_start(out_words[:, cols], oq[:, cols])
+
+        for c in range(2):
+            a, b = c * half, (c + 1) * half
             for t in range(PACK):
-                nc.vector.tensor_tensor(prod[:, t, :], h_w[t][:].indirect(n6_sb[:, a // 16 : b // 16]), t4[t][:, a:b], MULT)
-            for t in range(PACK):
-                nc.vector.tensor_tensor(res[:, t, :], tab_w[t][:].indirect(n5_sb[:, a // 16 : b // 16]), prod[:, t, :], ADD)
-                nc.sync.dma_start(out_rows[:, t, a:b], res[:, t, :])
-            dst = ob[:].rearrange("p (c i) t -> p c t i", i=4)
-            src = res[:].rearrange("p t (c i) -> p c t i", i=4)
-            if c + 1 < len(OUT_CHUNKS):
-                nc.scalar.copy(dst, src)
-            else:
-                nc.vector.tensor_copy(dst, src)
-            nc.vector.quantize_mx(out=oq[:, a:b].bitcast(FP8X4), scales=osc[:, a:b], in_=ob[:].rearrange("p s t -> p (s t)"))
-            nc.sync.dma_start(out_words[:, a:b], oq[:, a:b])
+                nc.vector.tensor_tensor(res[c][:, t, :], tab_w[t][:].indirect(n5_sb[:, a // 16 : b // 16]), prod[:, t, a:b], ADD)
+                nc.sync.dma_start(out_rows[:, t, a:b], res[c][:, t, :])
+        weave(nc.scalar.copy, 0, 0, half)
+        quantize_out(0)
+        weave(nc.scalar.copy, 1, 0, half // 2)
+        weave(nc.vector.tensor_copy, 1, half // 2, half)
+        quantize_out(1)
         for q in range(4):
             eng = nc.scalar if q % 2 else nc.sync
             eng.dma_start(out_2[0, 4 * q : 4 * q + 4, :].bitcast(I32), osc[32 * q : 32 * q + 4, :].bitcast(I32))

@@ -1,6 +1,7 @@
 from contextlib import ExitStack
 
 import concourse.mybir as mybir
+from concourse.masks import make_identity
 
 K, T, S, H, G, J = 512, 2048, 512, 512, 2048, 512
 FLOPS = 2 * K * H * S + 2 * H * H * S
@@ -21,7 +22,7 @@ SIGMOID = mybir.ActivationFunctionType.Sigmoid
 P = 128
 PACK = 4
 WINDOW = 1024
-OUT_CHUNKS = ((0, 256), (256, 512))
+SCALED_ON_VECTOR = 2
 
 
 def tile_picked_densewsumkinda_none_po_kernel(
@@ -38,13 +39,13 @@ def tile_picked_densewsumkinda_none_po_kernel(
             return lists.tile([P, S // 16], U16, name=name)
 
         def tiles(name, shape, dtype):
-            return [keep.tile(shape, dtype, name=name + str(t), align_bytes=64) for t in range(PACK)]
+            return [keep.tile(shape, dtype, name=name + str(t), tag=name + str(t), align_bytes=64) for t in range(PACK)]
 
         offs_sb, k1_sb = list_tile("offs_sb"), list_tile("k1_sb")
         n1_sb, n2_sb, n3_sb = list_tile("n1_sb"), list_tile("n2_sb"), list_tile("n3_sb")
         n4_sb, n5_sb, n6_sb = list_tile("n4_sb"), list_tile("n5_sb"), list_tile("n6_sb")
 
-        xw = keep.tile([P, T], I32, tag="xw", align_bytes=64)
+        xw = keep.tile([P, T], I32, align_bytes=64)
         xs = keep.tile([P, T], U8, align_bytes=64)
         w1w = keep.tile([P, 2 * H], U8, align_bytes=64)
         w1s = keep.tile([P, H], U8, align_bytes=64)
@@ -64,48 +65,47 @@ def tile_picked_densewsumkinda_none_po_kernel(
         nc.vector.memset(warm[:, 0:1], 0.0)
         nc.scalar.activation(warm[:, 1:2], warm[:, 0:1], SIGMOID)
         tab_rows = tab.rearrange("(p t) j -> p t j", t=PACK)
-        nc.sync.dma_start(n4_sb[:], n4)
         nc.sync.dma_start(tab_w[0][:, :J], tab_rows[:, 0, :])
-        nc.sync.dma_start(w1w[:].bitcast(I32), w1_words[0].bitcast(I32))
-        nc.sync.dma_start(tab_w[1][:, :J], tab_rows[:, 1, :])
-        nc.sync.dma_start(offs_sb[:], offs)
-        nc.sync.dma_start(xw[:], x_words[0].rearrange("p n t -> p (n t)").bitcast(I32))
         for q in range(4):
             nc.sync.dma_start(xs[32 * q : 32 * q + 4, :].bitcast(I32), x_scales[0, 4 * q : 4 * q + 4, :].bitcast(I32))
+        nc.sync.dma_start(n4_sb[:], n4)
+        nc.sync.dma_start(offs_sb[:], offs)
+        nc.sync.dma_start(xw[:], x_words[0].rearrange("p n t -> p (n t)").bitcast(I32))
+        nc.sync.dma_start(w1w[:].bitcast(I32), w1_words[0].bitcast(I32))
         for q in range(4):
             nc.sync.dma_start(w1s[32 * q : 32 * q + 4, :].bitcast(I32), w1_scales[0, 4 * q : 4 * q + 4, :].bitcast(I32))
         nc.gpsimd.dma_start(gs_sb[:], gs.rearrange("(p t) o -> p (t o)", t=PACK))
         for e in range(2):
             nc.gpsimd.dma_start(ds[e:P:16, :].bitcast(I32), d_scales[0, e:16:2, :].bitcast(I32))
-        nc.sync.dma_start(tab_w[2][:, :J], tab_rows[:, 2, :])
         nc.sync.dma_start(k1_sb[:], k1)
         nc.sync.dma_start(n1_sb[:], n1)
         nc.sync.dma_start(n3_sb[:], n3)
-        nc.sync.dma_start(dw[:], d_words[0].rearrange("p n t -> p (n t)").bitcast(I32))
         nc.sync.dma_start(n2_sb[:], n2)
+        nc.sync.dma_start(dw[:], d_words[0].rearrange("p n t -> p (n t)").bitcast(I32))
+        nc.sync.dma_start(tab_w[1][:, :J], tab_rows[:, 1, :])
+        nc.sync.dma_start(tab_w[2][:, :J], tab_rows[:, 2, :])
         nc.sync.dma_start(tab_w[3][:, :J], tab_rows[:, 3, :])
         nc.sync.dma_start(n6_sb[:], n6)
         nc.sync.dma_start(n5_sb[:], n5)
 
+        ident = keep.tile([P, P], F32, align_bytes=64)
+        make_identity(nc, ident[:])
         xsg = keep.tile([P, S], U8, align_bytes=64)
         xg = keep.tile([P, S], U32, align_bytes=64)
         w1d = keep.tile([P, 2 * H], U8, align_bytes=64)
         w1sd = keep.tile([P, H], U8, align_bytes=64)
-        t4_early = [keep.tile([P, S], F32, name="t4_" + str(t), align_bytes=64) for t in range(2)]
-        nc.vector.tensor_copy(t4_early[0][:], tab_w[0][:].indirect(n4_sb[:]))
+        t4_first = keep.tile([P, S], F32, align_bytes=64)
+        nc.vector.tensor_copy(t4_first[:], tab_w[0][:].indirect(n4_sb[:]))
+        nc.vector.tensor_copy(xsg[:], xs[:].indirect(offs_sb[:]))
+        nc.vector.tensor_copy(xg[:], xw[:].bitcast(U32).indirect(offs_sb[:]))
         nc.vector.tensor_copy(
             w1d[:].rearrange("p (t c i b) -> p c t i b", t=PACK, i=8, b=2),
             w1w[:].rearrange("p (c i t b) -> p c t i b", t=PACK, i=8, b=2),
         )
-        nc.vector.tensor_copy(t4_early[1][:], tab_w[1][:].indirect(n4_sb[:]))
-        nc.vector.tensor_copy(xg[:], xw[:].bitcast(U32).indirect(offs_sb[:]))
-        nc.vector.tensor_copy(xsg[:], xs[:].indirect(offs_sb[:]))
         nc.vector.tensor_copy(
             w1sd[:].rearrange("p (t c i) -> p c t i", t=PACK, i=16),
             w1s[:].rearrange("p (c i t) -> p c t i", t=PACK, i=16),
         )
-        t4_early.append(keep.tile([P, S], F32, name="t4_2", tag="xw", align_bytes=64))
-        nc.vector.tensor_copy(t4_early[2][:], tab_w[2][:].indirect(n4_sb[:]))
         y_ps = [psum.tile([P, S], F32, name="y_ps", tag="bank" + str(t)) for t in range(PACK)]
         for t in range(PACK):
             nc.tensor.matmul_mx(
@@ -121,8 +121,6 @@ def tile_picked_densewsumkinda_none_po_kernel(
         s3 = tiles("s3", [P, S], F32)
         term_a = keep.tile([P, PACK, S], F32, align_bytes=64)
         term_b = keep.tile([P, PACK, S], F32, align_bytes=64)
-        t4 = [t4_early[0][:], t4_early[1][:], t4_early[2][:], term_a[:, 0, :]]
-        dg = keep.tile([P, H], U32, align_bytes=64)
         dsg = keep.tile([P, H], U8, align_bytes=64)
         dd = keep.tile([P, H], I32, align_bytes=64)
         dsd = keep.tile([P, H], U8, align_bytes=64)
@@ -130,49 +128,82 @@ def tile_picked_densewsumkinda_none_po_kernel(
         sig = tiles("sig", [P, S], F32)
         for t in range(PACK):
             nc.scalar.activation(y_w[t][:, :S], y_ps[t][:], COPY)
-            nc.scalar.activation(yg_w[t][:, :S], y_ps[t][:], COPY, scale=gs_sb[:, t : t + 1])
+            if t >= SCALED_ON_VECTOR:
+                nc.scalar.activation(yg_w[t][:, :S], y_ps[t][:], COPY, scale=gs_sb[:, t : t + 1])
             nc.scalar.activation(sig[t][:], y_ps[t][:], SIGMOID)
             nc.scalar.activation(s3[t][:], y_w[t][:].indirect(n3_sb[:]), SIGMOID)
-            nc.vector.tensor_tensor(term_a[:, t, :], yg_w[t][:].indirect(n1_sb[:]), sig[t][:], MULT)
-            nc.vector.tensor_tensor(term_b[:, t, :], yg_w[t][:].indirect(n2_sb[:]), s3[t][:], MULT)
-
         nc.vector.tensor_copy(dsg[:], ds[:].indirect(k1_sb[:]))
-        nc.vector.tensor_copy(dg[:], dw[:].bitcast(U32).indirect(k1_sb[:]))
         nc.vector.tensor_copy(
             dsd[:].rearrange("p (t c i) -> p c t i", t=PACK, i=16),
             dsg[:].rearrange("p (c i t) -> p c t i", t=PACK, i=16),
-        )
-        nc.vector.tensor_copy(
-            dd[:].rearrange("p (t c i) -> p c t i", t=PACK, i=4),
-            dg[:].bitcast(I32).rearrange("p (c i t) -> p c t i", t=PACK, i=4),
         )
         for r in range(4):
             first = 16 * (r // 2) + r % 2
             nc.sync.dma_start(dsf[r:P:32, :].bitcast(I32), dsd[first:P:32, :].bitcast(I32))
 
-        zb = keep.tile([P, S, PACK], BF16, align_bytes=64)
+        zt_ps = [psum.tile([P, PACK, P], F32, name="zt_ps", tag="bank" + str(PACK + c)) for c in range(PACK)]
+
+        def turn(term, t, first):
+            for c in range(PACK):
+                nc.tensor.matmul(
+                    zt_ps[c][:, t, :], term[:, t, P * c : P * (c + 1)], ident[:],
+                    is_transpose=True, start=first, stop=not first,
+                )
+
+        def scale_on_vector(t):
+            nc.vector.tensor_scalar_mul(yg_w[t][:, :S], y_w[t][:, :S], gs_sb[:, t : t + 1])
+
+        scale_on_vector(0)
+        for t in range(PACK):
+            nc.vector.tensor_tensor(term_a[:, t, :], yg_w[t][:].indirect(n1_sb[:]), sig[t][:], MULT)
+            turn(term_a, t, True)
+            if t + 1 < SCALED_ON_VECTOR:
+                scale_on_vector(t + 1)
+            nc.vector.tensor_tensor(term_b[:, t, :], yg_w[t][:].indirect(n2_sb[:]), s3[t][:], MULT)
+            turn(term_b, t, False)
+
+        dg = keep.tile([P, H], U32, tag="s3" + str(PACK - 1), align_bytes=64)
+        t4_mid = keep.tile([P, 2, S], F32, tag="yg_w" + str(PACK - 1), align_bytes=64)
+        nc.vector.tensor_copy(dg[:], dw[:].bitcast(U32).indirect(k1_sb[:]))
+        nc.vector.tensor_copy(t4_mid[:, 0, :], tab_w[1][:].indirect(n4_sb[:]))
+        nc.vector.tensor_copy(
+            dd[:].rearrange("p (t c i) -> p c t i", t=PACK, i=4),
+            dg[:].bitcast(I32).rearrange("p (c i t) -> p c t i", t=PACK, i=4),
+        )
+        nc.vector.tensor_copy(t4_mid[:, 1, :], tab_w[2][:].indirect(n4_sb[:]))
+
+        half = S // 2
         zq = keep.tile([P, S], U32, align_bytes=64)
         zs = keep.tile([P, S], U8, align_bytes=64)
-        half = S // 2
-        for a in (0, half):
-            nc.vector.tensor_tensor(
-                zb[:, a : a + half, :].rearrange("p (c i) t -> p c t i", i=4),
-                term_a[:, :, a : a + half].rearrange("p t (c i) -> p c t i", i=4),
-                term_b[:, :, a : a + half].rearrange("p t (c i) -> p c t i", i=4),
-                ADD,
+        zr = tiles("zr", [P, H], BF16)
+        zb = [keep.tile([P, half, PACK], BF16, name="zb", tag="zb" + str(i), align_bytes=64) for i in range(2)]
+        for c in range(PACK):
+            nc.scalar.copy(
+                zr[c][:].rearrange("s (u p e) -> s u p e", u=2, e=2),
+                zt_ps[c][:].rearrange("s (u e) p -> s u p e", u=2),
             )
-        for a in (0, half):
+        for i in range(2):
+            xt_ps = psum.tile([P, 2, 2, P], F32, name="xt_ps", tag="bank" + str(i))
+            for cc in range(2):
+                words = zr[2 * i + cc][:].bitcast(F32)
+                for u in range(2):
+                    nc.tensor.transpose(xt_ps[:, cc, u, :], words[:, P * u : P * (u + 1)], ident[:])
+            nc.scalar.copy(
+                zb[i][:].rearrange("p s t -> p (s t)").bitcast(F32).rearrange("p (c s u) -> p c s u", c=2, u=2),
+                xt_ps[:].rearrange("p c u s -> p c s u"),
+            )
             nc.vector.quantize_mx(
-                out=zq[:, a : a + half].bitcast(FP8X4),
-                scales=zs[:, a : a + half],
-                in_=zb[:, a : a + half, :].rearrange("p s t -> p (s t)"),
+                out=zq[:, i * half : (i + 1) * half].bitcast(FP8X4),
+                scales=zs[:, i * half : (i + 1) * half],
+                in_=zb[i][:].rearrange("p s t -> p (s t)"),
             )
-        for t in (3,):
-            nc.vector.tensor_copy(t4[t], tab_w[t][:].indirect(n4_sb[:]))
+        t4_last = keep.tile([P, S], F32, tag="zb1", align_bytes=64)
+        nc.vector.tensor_copy(t4_last[:], tab_w[3][:].indirect(n4_sb[:]))
+        t4 = [t4_first[:], t4_mid[:, 0, :], t4_mid[:, 1, :], t4_last[:]]
 
         pieces = [(0, 0, half), (0, half, S)] + [(t, 0, S) for t in range(1, PACK)]
         for i, (t, a, b) in enumerate(pieces):
-            h_ps = psum.tile([P, S], F32, name="h_ps", tag="bank" + str((i + PACK) % 8))
+            h_ps = psum.tile([P, S], F32, name="h_ps", tag="bank" + str(i + 2))
             nc.tensor.matmul_mx(
                 out=h_ps[:, a:b],
                 lhsT=dd[:, P * t : P * (t + 1)].bitcast(FP8X4),

from contextlib import ExitStack

import concourse.mybir as mybir
from concourse.masks import make_identity

K, T, S, H, G, J = 512, 2048, 512, 512, 2048, 512
FLOPS = 2 * K * H * S + 2 * H * H * S

F32 = mybir.dt.float32
BF16 = mybir.dt.bfloat16
I32 = mybir.dt.int32
U32 = mybir.dt.uint32
U16 = mybir.dt.uint16
U8 = mybir.dt.uint8
FP8X4 = mybir.dt.float8_e4m3fn_x4
FP4X4 = mybir.dt.float4_e2m1fn_x4
MULT = mybir.AluOpType.mult
ADD = mybir.AluOpType.add
COPY = mybir.ActivationFunctionType.Copy
SIGMOID = mybir.ActivationFunctionType.Sigmoid

P = 128
PACK = 4
WINDOW = 1024
SCALED_ON_VECTOR = 2


def tile_picked_densewsumkinda_none_po_kernel(
    tc, x_words, x_scales, w1_words, w1_scales, gs, d_words, d_scales, tab,
    offs, n1, n2, n3, k1, n4, n5, n6, out_0, out_1, out_2,
):
    nc = tc.nc
    with ExitStack() as ctx:
        lists = ctx.enter_context(tc.tile_pool(name="lists", bufs=1))
        keep = ctx.enter_context(tc.tile_pool(name="keep", bufs=1))
        psum = ctx.enter_context(tc.psum_pool(name="psum", bufs=1))

        def list_tile(name):
            return lists.tile([P, S // 16], U16, name=name)

        def tiles(name, shape, dtype):
            return [keep.tile(shape, dtype, name=name + str(t), tag=name + str(t), align_bytes=64) for t in range(PACK)]

        offs_sb, k1_sb = list_tile("offs_sb"), list_tile("k1_sb")
        n1_sb, n2_sb, n3_sb = list_tile("n1_sb"), list_tile("n2_sb"), list_tile("n3_sb")
        n4_sb, n5_sb, n6_sb = list_tile("n4_sb"), list_tile("n5_sb"), list_tile("n6_sb")

        xw = keep.tile([P, T], I32, align_bytes=64)
        xs = keep.tile([P, T], U8, align_bytes=64)
        w1w = keep.tile([P, 2 * H], U8, align_bytes=64)
        w1s = keep.tile([P, H], U8, align_bytes=64)
        dw = keep.tile([P, G], I32, align_bytes=64)
        ds = keep.tile([P, G], U8, align_bytes=64)
        dsf = keep.tile([P, H], U8, align_bytes=64)
        gs_sb = keep.tile([P, PACK], F32, align_bytes=64)
        warm = keep.tile([P, 2], F32, align_bytes=64)
        tab_w = tiles("tab_w", [P, WINDOW], F32)
        y_w = tiles("y_w", [P, WINDOW], F32)
        yg_w = tiles("yg_w", [P, WINDOW], F32)
        h_w = tiles("h_w", [P, WINDOW], F32)

        nc.vector.memset(xs[:].bitcast(I32), 0)
        nc.vector.memset(w1s[:].bitcast(I32), 0)
        nc.gpsimd.memset(ds[:].bitcast(I32), 0)
        nc.vector.memset(warm[:, 0:1], 0.0)
        nc.scalar.activation(warm[:, 1:2], warm[:, 0:1], SIGMOID)
        tab_rows = tab.rearrange("(p t) j -> p t j", t=PACK)
        nc.sync.dma_start(tab_w[0][:, :J], tab_rows[:, 0, :])
        for q in range(4):
            nc.sync.dma_start(xs[32 * q : 32 * q + 4, :].bitcast(I32), x_scales[0, 4 * q : 4 * q + 4, :].bitcast(I32))
        nc.sync.dma_start(n4_sb[:], n4)
        nc.sync.dma_start(offs_sb[:], offs)
        nc.sync.dma_start(xw[:], x_words[0].rearrange("p n t -> p (n t)").bitcast(I32))
        nc.sync.dma_start(w1w[:].bitcast(I32), w1_words[0].bitcast(I32))
        for q in range(4):
            nc.sync.dma_start(w1s[32 * q : 32 * q + 4, :].bitcast(I32), w1_scales[0, 4 * q : 4 * q + 4, :].bitcast(I32))
        nc.gpsimd.dma_start(gs_sb[:], gs.rearrange("(p t) o -> p (t o)", t=PACK))
        for e in range(2):
            nc.gpsimd.dma_start(ds[e:P:16, :].bitcast(I32), d_scales[0, e:16:2, :].bitcast(I32))
        nc.sync.dma_start(k1_sb[:], k1)
        nc.sync.dma_start(n1_sb[:], n1)
        nc.sync.dma_start(n3_sb[:], n3)
        nc.sync.dma_start(n2_sb[:], n2)
        nc.sync.dma_start(dw[:], d_words[0].rearrange("p n t -> p (n t)").bitcast(I32))
        nc.sync.dma_start(tab_w[1][:, :J], tab_rows[:, 1, :])
        nc.sync.dma_start(tab_w[2][:, :J], tab_rows[:, 2, :])
        nc.sync.dma_start(tab_w[3][:, :J], tab_rows[:, 3, :])
        nc.sync.dma_start(n6_sb[:], n6)
        nc.sync.dma_start(n5_sb[:], n5)

        ident = keep.tile([P, P], F32, align_bytes=64)
        make_identity(nc, ident[:])
        xsg = keep.tile([P, S], U8, align_bytes=64)
        xg = keep.tile([P, S], U32, align_bytes=64)
        w1d = keep.tile([P, 2 * H], U8, align_bytes=64)
        w1sd = keep.tile([P, H], U8, align_bytes=64)
        t4_first = keep.tile([P, S], F32, align_bytes=64)
        nc.vector.tensor_copy(t4_first[:], tab_w[0][:].indirect(n4_sb[:]))
        nc.vector.tensor_copy(xsg[:], xs[:].indirect(offs_sb[:]))
        nc.vector.tensor_copy(xg[:], xw[:].bitcast(U32).indirect(offs_sb[:]))
        nc.vector.tensor_copy(
            w1d[:].rearrange("p (t c i b) -> p c t i b", t=PACK, i=8, b=2),
            w1w[:].rearrange("p (c i t b) -> p c t i b", t=PACK, i=8, b=2),
        )
        nc.vector.tensor_copy(
            w1sd[:].rearrange("p (t c i) -> p c t i", t=PACK, i=16),
            w1s[:].rearrange("p (c i t) -> p c t i", t=PACK, i=16),
        )
        y_ps = [psum.tile([P, S], F32, name="y_ps", tag="bank" + str(t)) for t in range(PACK)]
        for t in range(PACK):
            nc.tensor.matmul_mx(
                out=y_ps[t][:],
                lhsT=w1d[:, 2 * P * t : 2 * P * (t + 1)].bitcast(FP4X4),
                lhsT_scale=w1sd[:, P * t : P * (t + 1)],
                rhs=xg[:].bitcast(FP8X4),
                rhs_scale=xsg[:],
                start=True,
                stop=True,
            )

        s3 = tiles("s3", [P, S], F32)
        term_a = keep.tile([P, PACK, S], F32, align_bytes=64)
        term_b = keep.tile([P, PACK, S], F32, align_bytes=64)
        dsg = keep.tile([P, H], U8, align_bytes=64)
        dd = keep.tile([P, H], I32, align_bytes=64)
        dsd = keep.tile([P, H], U8, align_bytes=64)

        sig = tiles("sig", [P, S], F32)
        for t in range(PACK):
            nc.scalar.activation(y_w[t][:, :S], y_ps[t][:], COPY)
            if t >= SCALED_ON_VECTOR:
                nc.scalar.activation(yg_w[t][:, :S], y_ps[t][:], COPY, scale=gs_sb[:, t : t + 1])
            nc.scalar.activation(sig[t][:], y_ps[t][:], SIGMOID)
            nc.scalar.activation(s3[t][:], y_w[t][:].indirect(n3_sb[:]), SIGMOID)
        nc.vector.tensor_copy(dsg[:], ds[:].indirect(k1_sb[:]))
        nc.vector.tensor_copy(
            dsd[:].rearrange("p (t c i) -> p c t i", t=PACK, i=16),
            dsg[:].rearrange("p (c i t) -> p c t i", t=PACK, i=16),
        )
        for r in range(4):
            first = 16 * (r // 2) + r % 2
            nc.sync.dma_start(dsf[r:P:32, :].bitcast(I32), dsd[first:P:32, :].bitcast(I32))

        zt_ps = [psum.tile([P, PACK, P], F32, name="zt_ps", tag="bank" + str(PACK + c)) for c in range(PACK)]

        def turn(term, t, first):
            for c in range(PACK):
                nc.tensor.matmul(
                    zt_ps[c][:, t, :], term[:, t, P * c : P * (c + 1)], ident[:],
                    is_transpose=True, start=first, stop=not first,
                )

        def scale_on_vector(t):
            nc.vector.tensor_scalar_mul(yg_w[t][:, :S], y_w[t][:, :S], gs_sb[:, t : t + 1])

        scale_on_vector(0)
        for t in range(PACK):
            nc.vector.tensor_tensor(term_a[:, t, :], yg_w[t][:].indirect(n1_sb[:]), sig[t][:], MULT)
            turn(term_a, t, True)
            if t + 1 < SCALED_ON_VECTOR:
                scale_on_vector(t + 1)
            nc.vector.tensor_tensor(term_b[:, t, :], yg_w[t][:].indirect(n2_sb[:]), s3[t][:], MULT)
            turn(term_b, t, False)

        dg = keep.tile([P, H], U32, tag="s3" + str(PACK - 1), align_bytes=64)
        t4_mid = keep.tile([P, 2, S], F32, tag="yg_w" + str(PACK - 1), align_bytes=64)
        nc.vector.tensor_copy(dg[:], dw[:].bitcast(U32).indirect(k1_sb[:]))
        nc.vector.tensor_copy(t4_mid[:, 0, :], tab_w[1][:].indirect(n4_sb[:]))
        nc.vector.tensor_copy(
            dd[:].rearrange("p (t c i) -> p c t i", t=PACK, i=4),
            dg[:].bitcast(I32).rearrange("p (c i t) -> p c t i", t=PACK, i=4),
        )
        nc.vector.tensor_copy(t4_mid[:, 1, :], tab_w[2][:].indirect(n4_sb[:]))

        half = S // 2
        zq = keep.tile([P, S], U32, align_bytes=64)
        zs = keep.tile([P, S], U8, align_bytes=64)
        zr = tiles("zr", [P, H], BF16)
        zb = [keep.tile([P, half, PACK], BF16, name="zb", tag="zb" + str(i), align_bytes=64) for i in range(2)]
        for c in range(PACK):
            nc.scalar.copy(
                zr[c][:].rearrange("s (u p e) -> s u p e", u=2, e=2),
                zt_ps[c][:].rearrange("s (u e) p -> s u p e", u=2),
            )
        for i in range(2):
            xt_ps = psum.tile([P, 2, 2, P], F32, name="xt_ps", tag="bank" + str(i))
            for cc in range(2):
                words = zr[2 * i + cc][:].bitcast(F32)
                for u in range(2):
                    nc.tensor.transpose(xt_ps[:, cc, u, :], words[:, P * u : P * (u + 1)], ident[:])
            nc.scalar.copy(
                zb[i][:].rearrange("p s t -> p (s t)").bitcast(F32).rearrange("p (c s u) -> p c s u", c=2, u=2),
                xt_ps[:].rearrange("p c u s -> p c s u"),
            )
            nc.vector.quantize_mx(
                out=zq[:, i * half : (i + 1) * half].bitcast(FP8X4),
                scales=zs[:, i * half : (i + 1) * half],
                in_=zb[i][:].rearrange("p s t -> p (s t)"),
            )
        t4_last = keep.tile([P, S], F32, tag="zb1", align_bytes=64)
        nc.vector.tensor_copy(t4_last[:], tab_w[3][:].indirect(n4_sb[:]))
        t4 = [t4_first[:], t4_mid[:, 0, :], t4_mid[:, 1, :], t4_last[:]]

        pieces = [(0, 0, half), (0, half, S)] + [(t, 0, S) for t in range(1, PACK)]
        for i, (t, a, b) in enumerate(pieces):
            h_ps = psum.tile([P, S], F32, name="h_ps", tag="bank" + str(i + 2))
            nc.tensor.matmul_mx(
                out=h_ps[:, a:b],
                lhsT=dd[:, P * t : P * (t + 1)].bitcast(FP8X4),
                lhsT_scale=dsf[:, P * t : P * (t + 1)],
                rhs=zq[:, a:b].bitcast(FP8X4),
                rhs_scale=zs[:, a:b],
                start=True,
                stop=True,
            )
            nc.scalar.activation(h_w[t][:, a:b], h_ps[:, a:b], COPY, scale=0.0625)

        prod = keep.tile([P, PACK, S], F32, align_bytes=64)
        for t in range(PACK):
            nc.vector.tensor_tensor(prod[:, t, :], h_w[t][:].indirect(n6_sb[:]), t4[t], MULT)
        out_rows = out_0.rearrange("(p t) s -> p t s", t=PACK)
        oq = keep.tile([P, S], I32, align_bytes=64)
        osc = keep.tile([P, S], U8, align_bytes=64)
        out_words = out_1[0].rearrange("p n t -> p (n t)").bitcast(I32)
        res = [keep.tile([P, PACK, half], F32, name="res" + str(c), align_bytes=64) for c in range(2)]
        ob = [keep.tile([P, half, PACK], BF16, name="ob" + str(c), align_bytes=64) for c in range(2)]

        def weave(copy, c, a, b):
            copy(
                ob[c][:, a:b, :].rearrange("p (g i) t -> p g t i", i=4),
                res[c][:, :, a:b].rearrange("p t (g i) -> p g t i", i=4),
            )

        def quantize_out(c):
            cols = slice(c * half, (c + 1) * half)
            nc.vector.quantize_mx(out=oq[:, cols].bitcast(FP8X4), scales=osc[:, cols], in_=ob[c][:].rearrange("p s t -> p (s t)"))
            nc.sync.dma_start(out_words[:, cols], oq[:, cols])

        for c in range(2):
            a, b = c * half, (c + 1) * half
            for t in range(PACK):
                nc.vector.tensor_tensor(res[c][:, t, :], tab_w[t][:].indirect(n5_sb[:, a // 16 : b // 16]), prod[:, t, a:b], ADD)
                nc.sync.dma_start(out_rows[:, t, a:b], res[c][:, t, :])
        weave(nc.scalar.copy, 0, 0, half)
        quantize_out(0)
        weave(nc.scalar.copy, 1, 0, half // 2)
        weave(nc.vector.tensor_copy, 1, half // 2, half)
        quantize_out(1)
        for q in range(4):
            eng = nc.scalar if q % 2 else nc.sync
            eng.dma_start(out_2[0, 4 * q : 4 * q + 4, :].bitcast(I32), osc[32 * q : 32 * q + 4, :].bitcast(I32))
